import numpy as np
import ml_dtypes

BF16 = ml_dtypes.bfloat16


def bf(x):
    return np.asarray(x, np.float32).astype(BF16)


def f32(x):
    return np.asarray(x, np.float32)


def f64(x):
    return np.asarray(x).astype(np.float64)


def striped(idx):
    return np.tile(idx.reshape(-1, 16).T, (8, 1))


def rows(idx, k):
    return np.tile(idx, (k, 1))


def look(tab, idx):
    return np.take_along_axis(f64(tab), rows(idx, len(tab)), axis=1)


K, S, V, N, M = 128, 2048, 1536, 1536, 512


def setup_inputs():
    return {"tab": f32(np.random.standard_normal((2, K, S))), "y": f32(np.random.standard_normal((K, V))), "w": bf(np.random.standard_normal((K, M)) / np.sqrt(K)), "b": f32(0.5 * np.random.standard_normal((M, 1))), "offs": striped(np.random.permutation(S)[:N])}


def reference(tab, y, w, b, offs):
    idx = offs[:16].T.reshape(-1)
    x = (look(tab[0], idx) + f64(y)) * (1.0 / (1.0 + np.exp(-look(tab[1], idx))))
    return np.maximum(f64(w).T @ x + f64(b), 0.0)

@@ -1,0 +1,57 @@
+import concourse.mybir as mybir
+
+F32, BF16, U16 = mybir.dt.float32, mybir.dt.bfloat16, mybir.dt.uint16
+ALU = mybir.AluOpType
+ACT = mybir.ActivationFunctionType
+
+P = 128
+PLACES = 2048
+N = 1536
+M = 512
+BLOCKS = M // P
+PIECE = 512
+LANES = 16
+
+FLOPS = 2 * P * M * N
+
+
+def tile_lookup_vg_addsig_relu_kernel(tc, tab, y, w, b, offs, out):
+    nc = tc.nc
+    out_rows = out.rearrange("(p c) i -> p c i", c=BLOCKS)
+    with (
+        tc.tile_pool(name="held", bufs=1) as held,
+        tc.tile_pool(name="work", bufs=N // PIECE) as work,
+        tc.psum_pool(name="psum", bufs=8) as psum,
+    ):
+        offsets = held.tile([P, N // LANES], U16, name="offsets")
+        gates = held.tile([P, PLACES], F32, name="gates")
+        values = held.tile([P, PLACES], F32, name="values")
+        stream = held.tile([P, N], F32, name="stream")
+        weights = held.tile([P, M], BF16, name="weights")
+        bias = held.tile([P, BLOCKS], F32, name="bias")
+        nc.sync.dma_start(offsets[:], offs)
+        nc.sync.dma_start(gates[:], tab[1])
+        nc.sync.dma_start(values[:], tab[0])
+        nc.sync.dma_start(stream[:], y)
+        nc.sync.dma_start(weights[:], w)
+        nc.sync.dma_start(bias[:], b.rearrange("(p c) one -> p (c one)", c=BLOCKS))
+        block_weights = weights[:].rearrange("r (p c) -> r c p", c=BLOCKS)
+
+        for start in range(0, N, PIECE):
+            cols = slice(start, start + PIECE)
+            picks = offsets[:, start // LANES : (start + PIECE) // LANES]
+            gate = work.tile([P, PIECE], F32, name="gate")
+            total = work.tile([P, PIECE], F32, name="total")
+            x = work.tile([P, PIECE], BF16, name="x")
+            nc.scalar.activation(gate[:], gates[:].indirect(picks), ACT.Sigmoid)
+            nc.vector.tensor_tensor(total[:], values[:].indirect(picks), stream[:, cols], ALU.add)
+            nc.vector.tensor_tensor(x[:], total[:], gate[:], ALU.mult)
+            for c in range(BLOCKS):
+                product = psum.tile([P, PIECE], F32, name="product")
+                result = work.tile([P, PIECE], F32, name=f"result{c}")
+                nc.tensor.matmul(product[:], block_weights[:, c, :], x[:], start=True, stop=True)
+                if c % 2 == 0:
+                    nc.scalar.activation(result[:], product[:], ACT.Relu, bias=bias[:, c : c + 1])
+                else:
+                    nc.vector.tensor_scalar(result[:], product[:], bias[:, c : c + 1], 0.0, ALU.add, ALU.max)
+                nc.sync.dma_start(out_rows[:, c, cols], result[:])

@@ -9,49 +9,69 @@ PLACES = 2048
 N = 1536
 M = 512
 BLOCKS = M // P
-PIECE = 512
 LANES = 16
+PIECES = (256, 256, 512, 512)
+assert sum(PIECES) == N
+SHARED = BLOCKS + 1
 
 FLOPS = 2 * P * M * N
 
 
 def tile_lookup_vg_addsig_relu_kernel(tc, tab, y, w, b, offs, out):
     nc = tc.nc
+    spans = [slice(sum(PIECES[:k]), sum(PIECES[: k + 1])) for k in range(len(PIECES))]
     out_rows = out.rearrange("(p c) i -> p c i", c=BLOCKS)
     with (
         tc.tile_pool(name="held", bufs=1) as held,
-        tc.tile_pool(name="work", bufs=N // PIECE) as work,
         tc.psum_pool(name="psum", bufs=8) as psum,
     ):
         offsets = held.tile([P, N // LANES], U16, name="offsets")
         gates = held.tile([P, PLACES], F32, name="gates")
         values = held.tile([P, PLACES], F32, name="values")
-        stream = held.tile([P, N], F32, name="stream")
         weights = held.tile([P, M], BF16, name="weights")
         bias = held.tile([P, BLOCKS], F32, name="bias")
-        nc.sync.dma_start(offsets[:], offs)
+        stream = held.tile([P, N], F32, name="stream")
+        gate = held.tile([P, N], F32, name="gate")
+        total = held.tile([P, N], F32, name="total")
+        x = held.tile([P, N], BF16, name="x")
+        result = held.tile([P, BLOCKS, N], F32, name="result")
+
+        warm_in = held.tile([P, 8], F32, name="warm_in")
+        warm_out = held.tile([P, 8], F32, name="warm_out")
+        nc.vector.memset(warm_in[:], 0.0)
+        nc.scalar.activation(warm_out[:], warm_in[:], ACT.Sigmoid)
+
         nc.sync.dma_start(gates[:], tab[1])
+        nc.sync.dma_start(offsets[:], offs)
         nc.sync.dma_start(values[:], tab[0])
-        nc.sync.dma_start(stream[:], y)
+        nc.sync.dma_start(stream[:, spans[0]], y[:, spans[0]])
         nc.sync.dma_start(weights[:], w)
         nc.sync.dma_start(bias[:], b.rearrange("(p c) one -> p (c one)", c=BLOCKS))
+        for span in spans[1:]:
+            nc.sync.dma_start(stream[:, span], y[:, span])
         block_weights = weights[:].rearrange("r (p c) -> r c p", c=BLOCKS)
 
-        for start in range(0, N, PIECE):
-            cols = slice(start, start + PIECE)
-            picks = offsets[:, start // LANES : (start + PIECE) // LANES]
-            gate = work.tile([P, PIECE], F32, name="gate")
-            total = work.tile([P, PIECE], F32, name="total")
-            x = work.tile([P, PIECE], BF16, name="x")
-            nc.scalar.activation(gate[:], gates[:].indirect(picks), ACT.Sigmoid)
-            nc.vector.tensor_tensor(total[:], values[:].indirect(picks), stream[:, cols], ALU.add)
-            nc.vector.tensor_tensor(x[:], total[:], gate[:], ALU.mult)
-            for c in range(BLOCKS):
-                product = psum.tile([P, PIECE], F32, name="product")
-                result = work.tile([P, PIECE], F32, name=f"result{c}")
-                nc.tensor.matmul(product[:], block_weights[:, c, :], x[:], start=True, stop=True)
-                if c % 2 == 0:
-                    nc.scalar.activation(result[:], product[:], ACT.Relu, bias=bias[:, c : c + 1])
-                else:
-                    nc.vector.tensor_scalar(result[:], product[:], bias[:, c : c + 1], 0.0, ALU.add, ALU.max)
-                nc.sync.dma_start(out_rows[:, c, cols], result[:])
+        def picks(cols):
+            return offsets[:, cols.start // LANES : cols.stop // LANES]
+
+        for span in spans:
+            nc.scalar.activation(gate[:, span], gates[:].indirect(picks(span)), ACT.Sigmoid)
+
+        for span in spans:
+            middle = (span.start + span.stop) // 2
+            halves = (slice(span.start, middle), slice(middle, span.stop))
+            for half in halves:
+                nc.vector.tensor_tensor(total[:, half], values[:].indirect(picks(half)), stream[:, half], ALU.add)
+            for half in halves:
+                nc.vector.tensor_tensor(x[:, half], total[:, half], gate[:, half], ALU.mult)
+
+        products = [(span, c) for span in spans for c in range(BLOCKS)]
+        for done, (span, c) in enumerate(products):
+            product = psum.tile([P, span.stop - span.start], F32, name="product")
+            nc.tensor.matmul(product[:], block_weights[:, c, :], x[:, span], start=True, stop=True)
+            left = len(products) - done
+            if left <= SHARED and (SHARED - left) % 2 == 0:
+                nc.vector.tensor_scalar(result[:, c, span], product[:], bias[:, c : c + 1], 0.0, ALU.add, ALU.max)
+            else:
+                nc.scalar.activation(result[:, c, span], product[:], ACT.Relu, bias=bias[:, c : c + 1])
+            nc.sync.dma_start(out_rows[:, c, span], result[:, c, span])

@@ -10,11 +10,17 @@ N = 1536
 M = 512
 BLOCKS = M // P
 LANES = 16
-PIECES = (256, 256, 512, 512)
+PSUM_BANKS = 8
+PIECES = (256, 320, 448, 512)
 assert sum(PIECES) == N
 SHARED = BLOCKS + 1
 
 FLOPS = 2 * P * M * N
+
+
+def halves(span):
+    middle = (span.start + span.stop) // 2
+    return slice(span.start, middle), slice(middle, span.stop)
 
 
 def tile_lookup_vg_addsig_relu_kernel(tc, tab, y, w, b, offs, out):
@@ -23,7 +29,8 @@ def tile_lookup_vg_addsig_relu_kernel(tc, tab, y, w, b, offs, out):
     out_rows = out.rearrange("(p c) i -> p c i", c=BLOCKS)
     with (
         tc.tile_pool(name="held", bufs=1) as held,
-        tc.psum_pool(name="psum", bufs=8) as psum,
+        tc.tile_pool(name="ring", bufs=2) as ring,
+        tc.psum_pool(name="psum", bufs=PSUM_BANKS) as psum,
     ):
         offsets = held.tile([P, N // LANES], U16, name="offsets")
         gates = held.tile([P, PLACES], F32, name="gates")
@@ -31,8 +38,7 @@ def tile_lookup_vg_addsig_relu_kernel(tc, tab, y, w, b, offs, out):
         weights = held.tile([P, M], BF16, name="weights")
         bias = held.tile([P, BLOCKS], F32, name="bias")
         stream = held.tile([P, N], F32, name="stream")
-        gate = held.tile([P, N], F32, name="gate")
-        total = held.tile([P, N], F32, name="total")
+        sigmoids = held.tile([P, N], F32, name="sigmoids")
         x = held.tile([P, N], BF16, name="x")
         result = held.tile([P, BLOCKS, N], F32, name="result")
 
@@ -55,15 +61,16 @@ def tile_lookup_vg_addsig_relu_kernel(tc, tab, y, w, b, offs, out):
             return offsets[:, cols.start // LANES : cols.stop // LANES]
 
         for span in spans:
-            nc.scalar.activation(gate[:, span], gates[:].indirect(picks(span)), ACT.Sigmoid)
+            nc.scalar.activation(sigmoids[:, span], gates[:].indirect(picks(span)), ACT.Sigmoid)
 
         for span in spans:
-            middle = (span.start + span.stop) // 2
-            halves = (slice(span.start, middle), slice(middle, span.stop))
-            for half in halves:
-                nc.vector.tensor_tensor(total[:, half], values[:].indirect(picks(half)), stream[:, half], ALU.add)
-            for half in halves:
-                nc.vector.tensor_tensor(x[:, half], total[:, half], gate[:, half], ALU.mult)
+            totals = []
+            for half in halves(span):
+                total = ring.tile([P, half.stop - half.start], F32, name="total")
+                nc.vector.tensor_tensor(total[:], values[:].indirect(picks(half)), stream[:, half], ALU.add)
+                totals.append(total)
+            for half, total in zip(halves(span), totals):
+                nc.vector.tensor_tensor(x[:, half], total[:], sigmoids[:, half], ALU.mult)
 
         products = [(span, c) for span in spans for c in range(BLOCKS)]
         for done, (span, c) in enumerate(products):

import concourse.mybir as mybir

F32, BF16, U16 = mybir.dt.float32, mybir.dt.bfloat16, mybir.dt.uint16
ALU = mybir.AluOpType
ACT = mybir.ActivationFunctionType

P = 128
PLACES = 2048
N = 1536
M = 512
BLOCKS = M // P
LANES = 16
PSUM_BANKS = 8
PIECES = (256, 320, 448, 512)
assert sum(PIECES) == N
SHARED = BLOCKS + 1

FLOPS = 2 * P * M * N


def halves(span):
    middle = (span.start + span.stop) // 2
    return slice(span.start, middle), slice(middle, span.stop)


def tile_lookup_vg_addsig_relu_kernel(tc, tab, y, w, b, offs, out):
    nc = tc.nc
    spans = [slice(sum(PIECES[:k]), sum(PIECES[: k + 1])) for k in range(len(PIECES))]
    out_rows = out.rearrange("(p c) i -> p c i", c=BLOCKS)
    with (
        tc.tile_pool(name="held", bufs=1) as held,
        tc.tile_pool(name="ring", bufs=2) as ring,
        tc.psum_pool(name="psum", bufs=PSUM_BANKS) as psum,
    ):
        offsets = held.tile([P, N // LANES], U16, name="offsets")
        gates = held.tile([P, PLACES], F32, name="gates")
        values = held.tile([P, PLACES], F32, name="values")
        weights = held.tile([P, M], BF16, name="weights")
        bias = held.tile([P, BLOCKS], F32, name="bias")
        stream = held.tile([P, N], F32, name="stream")
        sigmoids = held.tile([P, N], F32, name="sigmoids")
        x = held.tile([P, N], BF16, name="x")
        result = held.tile([P, BLOCKS, N], F32, name="result")

        warm_in = held.tile([P, 8], F32, name="warm_in")
        warm_out = held.tile([P, 8], F32, name="warm_out")
        nc.vector.memset(warm_in[:], 0.0)
        nc.scalar.activation(warm_out[:], warm_in[:], ACT.Sigmoid)

        nc.sync.dma_start(gates[:], tab[1])
        nc.sync.dma_start(offsets[:], offs)
        nc.sync.dma_start(values[:], tab[0])
        nc.sync.dma_start(stream[:, spans[0]], y[:, spans[0]])
        nc.sync.dma_start(weights[:], w)
        nc.sync.dma_start(bias[:], b.rearrange("(p c) one -> p (c one)", c=BLOCKS))
        for span in spans[1:]:
            nc.sync.dma_start(stream[:, span], y[:, span])
        block_weights = weights[:].rearrange("r (p c) -> r c p", c=BLOCKS)

        def picks(cols):
            return offsets[:, cols.start // LANES : cols.stop // LANES]

        for span in spans:
            nc.scalar.activation(sigmoids[:, span], gates[:].indirect(picks(span)), ACT.Sigmoid)

        for span in spans:
            totals = []
            for half in halves(span):
                total = ring.tile([P, half.stop - half.start], F32, name="total")
                nc.vector.tensor_tensor(total[:], values[:].indirect(picks(half)), stream[:, half], ALU.add)
                totals.append(total)
            for half, total in zip(halves(span), totals):
                nc.vector.tensor_tensor(x[:, half], total[:], sigmoids[:, half], ALU.mult)

        products = [(span, c) for span in spans for c in range(BLOCKS)]
        for done, (span, c) in enumerate(products):
            product = psum.tile([P, span.stop - span.start], F32, name="product")
            nc.tensor.matmul(product[:], block_weights[:, c, :], x[:, span], start=True, stop=True)
            left = len(products) - done
            if left <= SHARED and (SHARED - left) % 2 == 0:
                nc.vector.tensor_scalar(result[:, c, span], product[:], bias[:, c : c + 1], 0.0, ALU.add, ALU.max)
            else:
                nc.scalar.activation(result[:, c, span], product[:], ACT.Relu, bias=bias[:, c : c + 1])
            nc.sync.dma_start(out_rows[:, c, span], result[:, c, span])
